import numpy as np
import ml_dtypes


def mxq(x, axis, fmt="e4m3"):
    dtype, down = {"e4m3": (ml_dtypes.float8_e4m3fn, 7), "e5m2": (ml_dtypes.float8_e5m2, 14)}[fmt]
    v = np.moveaxis(np.asarray(x, np.float32).astype(ml_dtypes.bfloat16).astype(np.float64), axis, -1)
    blocks = v.reshape(v.shape[:-1] + (-1, 32))
    amax = np.abs(blocks).max(-1, keepdims=True)
    byte = np.maximum(np.where(amax > 0, np.frexp(amax)[1] - 1 + 127, 0) - down, 1)
    scale = np.exp2(byte - 127.0)
    codes = (blocks / scale).astype(np.float32).astype(dtype).astype(np.float64)
    return np.moveaxis((codes * scale).reshape(v.shape), -1, axis)


WIDE = False


def mx_kscale(k):
    if not WIDE:
        return np.ones(k)
    levels = np.array([10, -10, 5, -5, 0])
    if k % 512:
        return np.exp2(np.random.permutation(np.resize(levels, k // 32))).repeat(32)
    a = np.empty((k // 512, 16))
    for p in range(k // 512):
        a[p, :8] = np.random.permutation(np.resize(levels, 8))
        for g in range(8):
            far = levels[np.abs(levels - a[p, g]) >= 10]
            a[p, g + 8] = far[np.random.randint(len(far))]
    return np.exp2(a.ravel()).repeat(32)


BF16 = ml_dtypes.bfloat16


def bf(x):
    return np.asarray(x, np.float32).astype(BF16)


def f64(x):
    return np.asarray(x).astype(np.float64)


E2M1 = np.array([0.0, 0.5, 1.0, 1.5, 2.0, 3.0, 4.0, 6.0, -0.0, -0.5, -1.0, -1.5, -2.0, -3.0, -4.0, -6.0])


def pack_weight(w, fmt):
    k, n = w.shape
    w = f64(bf(w)).reshape(k // 32, 32, n)
    amax = np.abs(w).max(1)
    if fmt == "e4m3":
        byte = np.frexp(amax)[1] - 1 + 127 - 7
    else:
        mant, ex = np.frexp(amax / 6.0)
        byte = np.where(mant > 0.5, ex, ex - 1) + 127
    byte = np.clip(np.where(amax > 0, byte, 1), 1, 254)
    scaled = (w * np.exp2(127.0 - byte)[:, None, :]).reshape(k, n).astype(np.float32)
    by_word = np.ascontiguousarray(scaled.reshape(k // 512, 128, 4, n).transpose(0, 1, 3, 2))
    if fmt == "e4m3":
        words = by_word.astype(ml_dtypes.float8_e4m3fn).view(np.uint8)
    else:
        c = by_word.astype(ml_dtypes.float4_e2m1fn).view(np.uint8) & 0xF
        words = c[..., 0::2] | (c[..., 1::2] << 4)
    return np.ascontiguousarray(words), np.ascontiguousarray(byte.astype(np.uint8).reshape(k // 512, 16, n))


def unpack_weight(words, scales, fmt):
    g, p, n, _ = words.shape
    if fmt == "e4m3":
        vals = np.ascontiguousarray(words).view(ml_dtypes.float8_e4m3fn).astype(np.float64)
    else:
        nib = np.empty((g, p, n, 4), np.uint8)
        nib[..., 0::2] = words & 0xF
        nib[..., 1::2] = words >> 4
        vals = E2M1[nib]
    vals = vals * np.repeat(np.exp2(scales.astype(np.float64) - 127.0), 8, axis=1)[..., None]
    return vals.transpose(0, 1, 3, 2).reshape(g * 512, n)
def pack4(w):
    words, scales = pack_weight(w, "e2m1")
    return words.reshape(words.shape[0], 128, -1), scales


def unpack4(words, scales):
    return unpack_weight(words.reshape(words.shape[0], 128, -1, 2), scales, "e2m1")


def planes(Y):
    n, m = Y.shape
    b = f64(bf(Y)).reshape(n // 32, 32, m)
    amax = np.abs(b).max(1)
    byte = np.clip(np.where(amax > 0, np.frexp(amax)[1] - 1 + 127 - 7, 1), 1, 254)
    codes = (b * np.exp2(127.0 - byte)[:, None, :]).reshape(n, m).astype(np.float32).astype(ml_dtypes.float8_e4m3fn).view(np.uint8)
    words = codes.reshape(n // 512, 128, 4, m).transpose(0, 1, 3, 2)
    return np.ascontiguousarray(words), np.ascontiguousarray(byte.astype(np.uint8).reshape(n // 512, 16, m))


F, K, O = 768, 1536, 1024

def setup_inputs():
    s = mx_kscale(K)
    x = np.random.randn(K, F) / np.sqrt(K) * s[:, None]
    x_words, x_scales = pack_weight(x, "e4m3")
    a_words, a_scales = pack4(np.random.randn(K, O) / s[:, None])
    b_words, b_scales = pack_weight(np.random.randn(K, O) / s[:, None], "e4m3")
    unit = np.exp(0.8 * np.random.randn(O))
    base0 = 0.5 * unit * np.random.randn(O)
    v = bf(base0 + unit * np.random.randn(K, O))
    base = bf(base0)
    w = bf(np.exp(0.3 * np.random.randn(K)) / s)
    return {"x_words": x_words, "x_scales": x_scales, "a_words": a_words, "a_scales": a_scales,
            "b_words": b_words, "b_scales": b_scales, "v": v, "base": base, "w": w}

def reference(x_words, x_scales, a_words, a_scales, b_words, b_scales, v, base, w):
    X = unpack_weight(x_words, x_scales, "e4m3")
    A = unpack4(a_words, a_scales)
    B = unpack_weight(b_words, b_scales, "e4m3")
    D = mxq(f64(w)[:, None] * (f64(v) - f64(base)), 0, "e4m3")
    phi_a = X.T @ A
    phi_b = X.T @ B
    phi_c = X.T @ D
    agree = 1.0 / (1.0 + np.exp(-(phi_a * phi_b)))
    y = phi_c * agree
    Y = y.T
    words, scales = planes(Y)
    return y, words, scales

from contextlib import ExitStack

import concourse.mybir as mybir
from concourse.masks import make_identity

F, K, O = 768, 1536, 1024
FLOPS = 3 * 2 * F * K * O

F32 = mybir.dt.float32
BF16 = mybir.dt.bfloat16
I32 = mybir.dt.int32
U32 = mybir.dt.uint32
U8 = mybir.dt.uint8
FP8X4 = mybir.dt.float8_e4m3fn_x4
FP4X4 = mybir.dt.float4_e2m1fn_x4
ACT = mybir.ActivationFunctionType
ALU = mybir.AluOpType

P = 128
PACK = 4
G = K // (P * PACK)
N = 512
H = O // N
FT = F // P
B_PLANE = 4


def tile_coalition_attribution_agreement_k3_kernel(
    tc, x_words, x_scales, a_words, a_scales, b_words, b_scales, v, base, w, out_0, out_1, out_2
):
    nc = tc.nc
    with ExitStack() as ctx:
        keep = ctx.enter_context(tc.tile_pool(name="keep", bufs=1))
        work = ctx.enter_context(tc.tile_pool(name="work", bufs=2))
        psum = ctx.enter_context(tc.psum_pool(name="psum", bufs=1))
        ctx.enter_context(tc.manual_schedule())

        def kept(name, shape, dtype):
            return keep.tile(shape, dtype, name=name, align_bytes=64)

        free_banks = [0, 1, 2, 3, 4, 5, 6, 7]
        held = {}

        def take_bank(key, shape):
            i = free_banks.pop(0)
            held[key] = i
            return psum.tile(shape, F32, name="bank%d" % i, tag="bank%d" % i)

        def give_bank(key):
            free_banks.append(held[key])

        xw = [kept("xw%d" % g, [P, F], U32) for g in range(G)]
        aw = [[kept("aw%d%d" % (h, g), [P, 2 * N], U8) for g in range(G)] for h in range(H)]
        bw = [[kept("bw%d%d" % (h, g), [P, N], U32) for g in range(G)] for h in range(H)]
        xs = kept("xs", [P, G, F], U8)
        as_ = kept("as_", [P, G, O], U8)
        bs = kept("bs", [P, G, O], U8)
        vt = [kept("vt%d" % q, [P, PACK, N], BF16) for q in range(H * G)]
        dw = [kept("dw%d" % q, [P, N], U32) for q in range(H * G)]
        ds = [kept("ds%d" % q, [P, N], U8) for q in range(H * G)]
        yw = [kept("yw%d" % h, [P, F], U32) for h in range(H)]
        ys = [kept("ys%d" % h, [P, F], U8) for h in range(H)]
        base_sb = kept("base_sb", [P, O // P], BF16)
        w_bf = kept("w_bf", [P, G, PACK], BF16)
        w32 = kept("w32", [P, G, PACK], F32)
        ident = kept("ident", [P, P], F32)
        warm = kept("warm", [P, 8], F32)
        gate = [kept("gate%d" % n, [P, N], F32) for n in range(H * FT)]

        state = {}

        def load_scales(queue, tile, scales, row0, quad):
            queue.dma_start(
                out=tile[32 * quad + row0 : 32 * quad + row0 + 4, :, :].bitcast(I32),
                in_=scales[:, 4 * quad : 4 * quad + 4, :].rearrange("g r n -> r g n").bitcast(I32),
            )

        def zero(tile):
            nc.vector.memset(tile[:].rearrange("p g n -> p (g n)").bitcast(I32), 0)

        def load_x(queue, g):
            queue.dma_start(out=xw[g][:].bitcast(I32), in_=x_words[g].rearrange("p n t -> p (n t)").bitcast(I32))

        def load_a(queue, h, g):
            queue.dma_start(out=aw[h][g][:].bitcast(I32), in_=a_words[g][:, 2 * N * h : 2 * N * (h + 1)].bitcast(I32))

        def load_b(queue, h, g):
            src = b_words[g].rearrange("p n t -> p (n t)")[:, 4 * N * h : 4 * N * (h + 1)]
            queue.dma_start(out=bw[h][g][:].bitcast(I32), in_=src.bitcast(I32))

        def load_v(queue, q):
            h, g = divmod(q, G)
            rows = v[P * PACK * g : P * PACK * (g + 1), N * h : N * (h + 1)]
            queue.dma_start(out=vt[q][:], in_=rows.rearrange("(p j) o -> p j o", j=PACK))

        def mx_pass(kind, n, g):
            h, f = divmod(n, FT)
            cols = slice(N * h, N * (h + 1))
            if kind == "a":
                rhs, rhs_scale = aw[h][g][:].bitcast(FP4X4), as_[:, g, cols]
            elif kind == "b":
                rhs, rhs_scale = bw[h][g][:].bitcast(FP8X4), bs[B_PLANE:P, g, cols]
            else:
                rhs, rhs_scale = dw[G * h + g][:].bitcast(FP8X4), ds[G * h + g][:]
            fc = slice(P * f, P * (f + 1))
            nc.tensor.matmul_mx(
                out=state[kind, n][:],
                lhsT=xw[g][:, fc].bitcast(FP8X4),
                lhsT_scale=xs[:, g, fc],
                rhs=rhs,
                rhs_scale=rhs_scale,
                start=(g == 0),
                stop=(g == G - 1),
            )

        def product(kind, n):
            state[kind, n] = take_bank((kind, n), [P, N])
            for g in range(G):
                mx_pass(kind, n, g)

        def copy_a(n, engine):
            if engine == "S":
                nc.scalar.copy(out=gate[n][:], in_=state["a", n][:])
            else:
                nc.vector.tensor_copy(out=gate[n][:], in_=state["a", n][:])
            give_bank(("a", n))

        def mul_ab(n):
            nc.vector.tensor_tensor(out=gate[n][:], in0=state["b", n][:], in1=gate[n][:], op=ALU.mult)
            give_bank(("b", n))

        def sigmoid(n):
            nc.scalar.activation(out=gate[n][:], in_=gate[n][:], func=ACT.Sigmoid)

        def sub(q, j):
            h = q // G
            state["diff", q, j] = work.tile([P, N], F32, name="diff", bufs=8)
            spread = state["base"][:].rearrange("p u n -> p (u n)").bitcast(BF16)
            spread = spread.rearrange("p (u n e) -> p n u e", u=4, e=2)[:, 64 * h : 64 * (h + 1), :, :]
            nc.vector.tensor_tensor(
                out=state["diff", q, j][:].rearrange("p (n u e) -> p n u e", u=4, e=2),
                in0=vt[q][:, j, :].rearrange("p (n u e) -> p n u e", u=4, e=2),
                in1=spread,
                op=ALU.subtract,
            )
            if (q, j) == (H * G - 1, PACK - 1):
                give_bank("base")

        def scale(q, j):
            g = q % G
            if j == 0:
                state["rows", q] = work.tile([P, PACK, N], BF16, name="rows", bufs=3)
            nc.scalar.activation(
                out=state["rows", q][:, j, :], in_=state["diff", q, j][:], func=ACT.Copy, scale=w32[:, g, j : j + 1]
            )

        def weave(q):
            state["woven", q] = work.tile([P, N, PACK], BF16, name="woven", bufs=1, align_bytes=64)
            nc.gpsimd.tensor_scalar(
                out=state["woven", q][:],
                in0=state["rows", q][:].rearrange("p j o -> p o j"),
                scalar1=1.0,
                scalar2=1.0,
                op0=ALU.mult,
                op1=ALU.mult,
            )

        def quant_d(q):
            nc.vector.quantize_mx(
                out=dw[q][:].bitcast(FP8X4), scales=ds[q][:], in_=state["woven", q][:].rearrange("p o j -> p (o j)")
            )

        def mul_c(n):
            h, f = divmod(n, FT)
            y = work.tile([P, N], F32, name="y", bufs=12)
            state["y", n] = y
            nc.vector.tensor_tensor(out=y[:], in0=state["c", n][:], in1=gate[n][:], op=ALU.mult)
            give_bank(("c", n))
            nc.sync.dma_start(out=out_0[P * f : P * (f + 1), N * h : N * (h + 1)], in_=y[:])

        def cast(n, engine):
            y16 = work.tile([P, 2, P, 2], BF16, name="y16", bufs=6)
            state["y16", n] = y16
            src = state["y", n][:].rearrange("f (p u e) -> f u p e", u=2, e=2)
            if engine == "S":
                nc.scalar.copy(out=y16[:], in_=src)
            elif engine == "G":
                nc.gpsimd.tensor_scalar(out=y16[:], in0=src, scalar1=1.0, scalar2=1.0, op0=ALU.mult, op1=ALU.mult)
            else:
                nc.vector.tensor_copy(out=y16[:], in_=src)

        def turn(tiles):
            turned = take_bank(tiles, [P, 2 * len(tiles), P])
            state["turned", tiles] = turned
            for s, n in enumerate(tiles):
                words = state["y16", n][:].rearrange("f u p e -> f (u p e)").bitcast(F32)
                for u in range(2):
                    nc.tensor.transpose(turned[:, 2 * s + u, :], words[:, P * u : P * (u + 1)], ident[:])

        def unturn(tiles):
            yq = work.tile([P, len(tiles) * N], BF16, name="yq", align_bytes=64)
            state["yq", tiles] = yq
            nc.scalar.copy(
                out=yq[:].bitcast(F32).rearrange("p (s f u) -> p s f u", f=P, u=2),
                in_=state["turned", tiles][:].rearrange("p (s u) f -> p s f u", u=2),
            )
            give_bank(tiles)

        def quant_y(tiles):
            h, f = divmod(tiles[0], FT)
            fc = slice(P * f, P * (f + len(tiles)))
            nc.vector.quantize_mx(out=yw[h][:, fc].bitcast(FP8X4), scales=ys[h][:, fc], in_=state["yq", tiles][:])
            store_codes(h, f, f + len(tiles))
            if f + len(tiles) == FT:
                store_scales(h, [nc.sync] * 4 if h == 0 else [nc.scalar, nc.sync, nc.scalar, nc.sync])

        def store_codes(h, f0, f1):
            dst = out_1[h].rearrange("p m t -> p (m t)").bitcast(I32)
            nc.sync.dma_start(out=dst[:, P * f0 : P * f1], in_=yw[h][:, P * f0 : P * f1].bitcast(I32))

        def store_scales(h, queues):
            for quad in range(4):
                queues[quad].dma_start(
                    out=out_2[h][4 * quad : 4 * quad + 4, :].bitcast(I32),
                    in_=ys[h][32 * quad : 32 * quad + 4, :].bitcast(I32),
                )

        zero(xs)
        zero(as_)
        nc.vector.memset(warm[:], 0.0)
        nc.scalar.activation(out=warm[:, 0:1], in_=warm[:, 0:1], func=ACT.Sigmoid)
        zero(bs)
        nc.gpsimd.dma_start(out=base_sb[:], in_=base.rearrange("(p c) -> p c", p=P))
        load_v(nc.gpsimd, 0)
        make_identity(nc, ident[:])
        load_x(nc.sync, 0)
        load_a(nc.sync, 0, 0)
        load_scales(nc.sync, xs, x_scales, 0, 0)
        load_scales(nc.sync, xs, x_scales, 0, 2)
        load_scales(nc.sync, xs, x_scales, 0, 1)
        load_scales(nc.sync, xs, x_scales, 0, 3)
        load_scales(nc.sync, as_, a_scales, 0, 0)
        load_scales(nc.sync, as_, a_scales, 0, 2)
        load_scales(nc.sync, as_, a_scales, 0, 1)
        load_scales(nc.sync, as_, a_scales, 0, 3)
        nc.sync.dma_start(out=w_bf[:], in_=w.rearrange("(g p j) -> p g j", p=P, j=PACK))
        load_x(nc.sync, 1)
        load_a(nc.sync, 0, 1)
        load_v(nc.sync, 1)
        load_x(nc.sync, 2)
        load_a(nc.sync, 0, 2)
        load_v(nc.sync, 2)
        load_scales(nc.sync, bs, b_scales, B_PLANE, 0)
        load_scales(nc.sync, bs, b_scales, B_PLANE, 2)
        load_scales(nc.sync, bs, b_scales, B_PLANE, 1)
        load_scales(nc.sync, bs, b_scales, B_PLANE, 3)
        load_b(nc.sync, 0, 0)
        load_b(nc.sync, 0, 1)
        load_b(nc.sync, 0, 2)
        load_a(nc.sync, 1, 0)
        load_a(nc.sync, 1, 1)
        load_a(nc.sync, 1, 2)
        load_v(nc.sync, 3)
        load_b(nc.sync, 1, 0)
        load_b(nc.sync, 1, 1)
        load_b(nc.sync, 1, 2)
        load_v(nc.sync, 4)
        load_v(nc.sync, 5)
        for n in range(FT):
            state["a", n] = take_bank(("a", n), [P, N])
        spare = free_banks.pop(0)
        state["base"] = take_bank("base", [P, 4, P])
        free_banks.append(spare)
        base_words = base_sb[:].bitcast(F32)
        for u in range(4):
            nc.tensor.transpose(state["base"][:, u, :], base_words[:, u : u + 1].to_broadcast([P, P]), ident[:])
        nc.vector.tensor_copy(out=w32[:], in_=w_bf[:])
        for g in range(G):
            for n in range(FT):
                mx_pass("a", n, g)
        sub(0, 0)
        sub(0, 1)
        sub(0, 2)
        scale(0, 0)
        sub(0, 3)
        sub(1, 0)
        sub(1, 1)
        sub(1, 2)
        sub(1, 3)
        sub(2, 0)
        scale(0, 1)
        scale(0, 2)
        scale(0, 3)
        sub(2, 1)
        sub(2, 2)
        weave(0)
        scale(1, 0)
        quant_d(0)
        product("b", 0)
        scale(1, 1)
        scale(1, 2)
        copy_a(0, "S")
        scale(1, 3)
        copy_a(1, "S")
        product("b", 1)
        product("b", 2)
        copy_a(2, "S")
        scale(2, 0)
        weave(1)
        product("b", 3)
        copy_a(3, "S")
        sub(2, 3)
        mul_ab(0)
        copy_a(4, "V")
        copy_a(5, "S")
        sigmoid(0)
        mul_ab(1)
        sub(3, 0)
        sub(3, 1)
        sub(3, 2)
        quant_d(1)
        product("a", 6)
        product("b", 4)
        product("a", 7)
        mul_ab(2)
        mul_ab(3)
        scale(2, 1)
        product("b", 5)
        mul_ab(4)
        mul_ab(5)
        scale(2, 2)
        scale(2, 3)
        scale(3, 0)
        sub(3, 3)
        sub(4, 0)
        copy_a(6, "S")
        scale(3, 1)
        weave(2)
        sigmoid(1)
        scale(3, 2)
        quant_d(2)
        product("a", 8)
        sub(4, 1)
        product("a", 9)
        copy_a(7, "S")
        product("b", 6)
        product("c", 0)
        sub(4, 2)
        copy_a(8, "S")
        sub(4, 3)
        sub(5, 0)
        product("c", 1)
        product("c", 2)
        scale(3, 3)
        mul_c(0)
        sigmoid(2)
        copy_a(9, "S")
        product("c", 3)
        sigmoid(3)
        mul_c(1)
        scale(4, 0)
        weave(3)
        quant_d(3)
        mul_ab(6)
        sub(5, 1)
        mul_c(2)
        sub(5, 2)
        sub(5, 3)
        scale(4, 1)
        scale(4, 2)
        product("b", 7)
        scale(4, 3)
        mul_c(3)
        product("a", 10)
        weave(4)
        sigmoid(4)
        quant_d(4)
        product("c", 4)
        cast(0, "S")
        scale(5, 0)
        scale(5, 1)
        cast(1, "V")
        mul_c(4)
        cast(2, "S")
        mul_ab(7)
        scale(5, 2)
        scale(5, 3)
        cast(3, "S")
        product("b", 8)
        product("b", 9)
        mul_ab(8)
        mul_ab(9)
        sigmoid(5)
        product("a", 11)
        turn((0, 1))
        unturn((0, 1))
        turn((2, 3))
        unturn((2, 3))
        copy_a(10, "V")
        weave(5)
        quant_y((0, 1))
        product("c", 5)
        quant_d(5)
        product("b", 10)
        product("b", 11)
        sigmoid(6)
        sigmoid(7)
        cast(4, "V")
        product("c", 6)
        product("c", 7)
        copy_a(11, "S")
        sigmoid(8)
        sigmoid(9)
        mul_ab(10)
        mul_c(5)
        product("c", 8)
        product("c", 9)
        product("c", 10)
        mul_c(6)
        sigmoid(10)
        mul_c(7)
        cast(5, "S")
        cast(6, "S")
        quant_y((2, 3))
        mul_ab(11)
        cast(7, "S")
        mul_c(8)
        turn((4, 5))
        turn((6, 7))
        sigmoid(11)
        unturn((4, 5))
        mul_c(9)
        mul_c(10)
        cast(8, "V")
        cast(9, "V")
        quant_y((4, 5))
        product("c", 11)
        mul_c(11)
        unturn((6, 7))
        quant_y((6, 7))
        cast(10, "S")
        turn((8, 9))
        turn((10,))
        cast(11, "V")
        turn((11,))
        unturn((8, 9))
        quant_y((8, 9))
        unturn((10,))
        quant_y((10,))
        unturn((11,))
        quant_y((11,))
